import numpy as np
import ml_dtypes


def mxq(x, axis, fmt="e4m3"):
    dtype, down = {"e4m3": (ml_dtypes.float8_e4m3fn, 7), "e5m2": (ml_dtypes.float8_e5m2, 14)}[fmt]
    v = np.moveaxis(np.asarray(x, np.float32).astype(ml_dtypes.bfloat16).astype(np.float64), axis, -1)
    blocks = v.reshape(v.shape[:-1] + (-1, 32))
    amax = np.abs(blocks).max(-1, keepdims=True)
    byte = np.maximum(np.where(amax > 0, np.frexp(amax)[1] - 1 + 127, 0) - down, 1)
    scale = np.exp2(byte - 127.0)
    codes = (blocks / scale).astype(np.float32).astype(dtype).astype(np.float64)
    return np.moveaxis((codes * scale).reshape(v.shape), -1, axis)


WIDE = False


def mx_kscale(k):
    if not WIDE:
        return np.ones(k)
    levels = np.array([10, -10, 5, -5, 0])
    if k % 512:
        return np.exp2(np.random.permutation(np.resize(levels, k // 32))).repeat(32)
    a = np.empty((k // 512, 16))
    for p in range(k // 512):
        a[p, :8] = np.random.permutation(np.resize(levels, 8))
        for g in range(8):
            far = levels[np.abs(levels - a[p, g]) >= 10]
            a[p, g + 8] = far[np.random.randint(len(far))]
    return np.exp2(a.ravel()).repeat(32)


def f64(x):
    return np.asarray(x).astype(np.float64)


def striped(idx):
    return np.tile(idx.reshape(-1, 16).T, (8, 1)).astype(np.uint16)


def unstriped(offs):
    return offs[:16].T.reshape(-1).astype(np.int64)


def pack_weight(w):
    k, n = w.shape
    w = f64(np.asarray(w, np.float32).astype(ml_dtypes.bfloat16)).reshape(k // 32, 32, n)
    amax = np.abs(w).max(1)
    byte = np.clip(np.where(amax > 0, np.frexp(amax)[1] - 1 + 127 - 7, 1), 1, 254)
    scaled = (w * np.exp2(127.0 - byte)[:, None, :]).reshape(k, n).astype(np.float32)
    words = np.ascontiguousarray(scaled.reshape(k // 512, 128, 4, n).transpose(0, 1, 3, 2)).astype(ml_dtypes.float8_e4m3fn).view(np.uint8)
    return words, np.ascontiguousarray(byte.astype(np.uint8).reshape(k // 512, 16, n))


def unpack_weight(words, scales):
    g, p, n, _ = words.shape
    vals = np.ascontiguousarray(words).view(ml_dtypes.float8_e4m3fn).astype(np.float64) * np.repeat(np.exp2(scales.astype(np.float64) - 127.0), 8, axis=1)[..., None]
    return vals.transpose(0, 1, 3, 2).reshape(g * 512, n)


def relu(v):
    return np.maximum(v, 0.0)


K, T, S, D, N, H, V, U = 1024, 2048, 1024, 4, 128, 512, 256, 512


def setup_inputs():
    n = np.random.standard_normal
    s = mx_kscale(K)[:, None]
    u = mx_kscale(H)
    packed_xT = pack_weight(n((K, T)) * s)
    return {
        "x_words": packed_xT[0],
        "x_scales": packed_xT[1],
        "w1": (n((K, H)) / np.sqrt(K) / s).astype(np.float32),
        "lod": (n((H, U))).astype(np.float32),
        "unit": (np.random.uniform(0.6, 1.4, (H, 1)) * u[:, None]).astype(np.float32),
        "w2": (n((H, N)) / np.sqrt(H) / u[:, None]).astype(np.float32),
        "offs": striped(np.random.permutation(T)[:S]),
        "par": striped(np.random.permutation(np.concatenate([np.arange(V), np.random.randint(0, V, U - V)]))),
        "nb": striped(np.random.permutation(U)),
    }


def reference(x_words, x_scales, w1, lod, unit, w2, offs, par, nb):
    xq = unpack_weight(x_words, x_scales)[:, unstriped(offs)]
    y = mxq(f64(w1), 0, "e4m3").T @ xq
    lev1 = y.reshape(len(y), -1, D).max(axis=2)
    lp = lev1[:, unstriped(par)]
    lev2 = lp + 0.7 * f64(lod)
    smo = 0.5 * (lev2 + lev2[:, unstriped(nb)])
    det = lev2 - smo
    hid = f64(unit) * (smo + relu(det))
    return mxq(f64(w2), 0, "e4m3").T @ mxq(hid, 0, "e4m3")

@@ -1,0 +1,229 @@
+from contextlib import ExitStack
+
+import concourse.mybir as mybir
+
+K, T, S, D, N, H, V, U = 1024, 2048, 1024, 4, 128, 512, 256, 512
+
+F32 = mybir.dt.float32
+BF16 = mybir.dt.bfloat16
+I32 = mybir.dt.int32
+U32 = mybir.dt.uint32
+U16 = mybir.dt.uint16
+U8 = mybir.dt.uint8
+FP8X4 = mybir.dt.float8_e4m3fn_x4
+ALU = mybir.AluOpType
+COPY = mybir.ActivationFunctionType.Copy
+AXIS_X = mybir.AxisListType.X
+
+FLOPS = 2 * K * H * S + 2 * H * N * U
+
+P = 128
+PACK = 4
+PASSES = K // (P * PACK)
+BANK = 512
+LIST = 16
+PAR_WINDOW = U + LIST
+STAGED = ()
+SMOOTH_WIDTH = 256
+CHUNKS = ((0, 256), (256, 128), (384, 128))
+
+
+def tile_picked_yoctree_relu_p_kernel(
+    tc, x_words, x_scales, w1, lod, unit, w2, offs, par, nb, out
+):
+    nc = tc.nc
+    halves = S // BANK
+
+    with ExitStack() as ctx:
+        keep = ctx.enter_context(tc.tile_pool(name="keep", bufs=1))
+        psum = ctx.enter_context(tc.psum_pool(name="psum", bufs=8))
+
+        offs_sb = keep.tile([P, S // LIST], U16, name="offs_sb")
+        par_sb = keep.tile([P, U // LIST], U16, name="par_sb")
+        nb_sb = keep.tile([P, U // LIST], U16, name="nb_sb")
+
+        x_table = [keep.tile([P, T], I32, name=f"x_table{o}") for o in range(PASSES)]
+        scale_table = keep.tile([P, T], U8, name="scale_table")
+        w1_raw = [[keep.tile([P, PACK, H // 2], F32, name=f"w1_raw{o}_{c}") for c in range(2)] for o in range(PASSES)]
+        lod_sb = [keep.tile([P, U], F32, name=f"lod_sb{t}") for t in range(PACK)]
+        unit_sb = keep.tile([P, PACK], F32, name="unit_sb")
+        w2_raw = keep.tile([P, PACK, N], F32, name="w2_raw")
+        lev1 = [keep.tile([P, 3 * V if t in STAGED else PAR_WINDOW], F32, name=f"lev1_{t}") for t in range(PACK)]
+
+        nc.vector.memset(scale_table[:].bitcast(I32), 0)
+        for t in range(PACK):
+            if t not in STAGED:
+                nc.vector.memset(lev1[t][:, V:], 0.0)
+
+        def load_x(o):
+            nc.sync.dma_start(out=x_table[o][:], in_=x_words[o].rearrange("p c r -> p (c r)").bitcast(I32))
+
+        def load_w1(o, c):
+            rows = w1[o * P * PACK : (o + 1) * P * PACK, c * (H // 2) : (c + 1) * (H // 2)]
+            nc.sync.dma_start(out=w1_raw[o][c][:], in_=rows.rearrange("(p j) c -> p j c", j=PACK))
+
+        nc.sync.dma_start(offs_sb[:], offs)
+        load_w1(0, 0)
+        nc.sync.dma_start(out=unit_sb[:], in_=unit.rearrange("(p t) one -> p (t one)", t=PACK))
+        for q in range(4):
+            nc.sync.dma_start(
+                out=scale_table[32 * q : 32 * q + 4 * PASSES, :].bitcast(I32),
+                in_=x_scales[:, 4 * q : 4 * q + 4, :].bitcast(I32),
+            )
+        load_x(0)
+        load_w1(0, 1)
+        load_x(1)
+        load_w1(1, 0)
+        load_w1(1, 1)
+        nc.sync.dma_start(out=w2_raw[:], in_=w2.rearrange("(p j) n -> p j n", j=PACK))
+        nc.sync.dma_start(par_sb[:], par)
+        lod_rows = lod.rearrange("(p t) r -> p t r", t=PACK)
+        for t in range(PACK):
+            nc.sync.dma_start(out=lod_sb[t][:], in_=lod_rows[:, t, :])
+        nc.sync.dma_start(nb_sb[:], nb)
+
+        x_scale = keep.tile([P, S], U8, name="x_scale", align_bytes=64)
+        x_code = [keep.tile([P, S], U32, name="x_code0", align_bytes=64)]
+        w1_bf = [keep.tile([P, PACK, P, PACK], BF16, name=f"w1_bf{o}", tag=f"w1_bf{o}", align_bytes=64) for o in range(PASSES)]
+        w1_code = [[keep.tile([P, P], U32, name=f"w1_code{o}_{t}", align_bytes=64) for t in range(PACK)] for o in range(PASSES)]
+        w1_scale = [[keep.tile([P, P], U8, name=f"w1_scale{o}_{t}", align_bytes=64) for t in range(PACK)] for o in range(PASSES)]
+        y = [[psum.tile([P, BANK], F32, name=f"y{t}_{h}", tag="bank") for h in range(halves)] for t in range(PACK)]
+
+        def gather_x(o):
+            nc.vector.tensor_copy(x_code[o][:], x_table[o][:].bitcast(U32).indirect(offs_sb[:]))
+
+        def round_w1(copy, o, c, m0, m1):
+            base = c * (P // 2)
+            copy(
+                w1_bf[o][:, :, base + m0 : base + m1, :].rearrange("p t m j -> p m j t"),
+                w1_raw[o][c][:, :, PACK * m0 : PACK * m1].rearrange("p j (m t) -> p m j t", t=PACK),
+            )
+
+        def quantize_w1(o, t):
+            nc.vector.quantize_mx(
+                out=w1_code[o][t][:].bitcast(FP8X4),
+                scales=w1_scale[o][t][:],
+                in_=w1_bf[o][:, t, :, :].rearrange("p m j -> p (m j)"),
+            )
+
+        def product(o, t):
+            for h in range(halves):
+                nc.tensor.matmul_mx(
+                    out=y[t][h][:],
+                    lhsT=w1_code[o][t][:].bitcast(FP8X4),
+                    lhsT_scale=w1_scale[o][t][:],
+                    rhs=x_code[o][:, h * BANK : (h + 1) * BANK].bitcast(FP8X4),
+                    rhs_scale=x_scale[4 * o :, h * BANK : (h + 1) * BANK],
+                    start=(o == 0),
+                    stop=(o == PASSES - 1),
+                )
+
+        nc.vector.tensor_copy(x_scale[:], scale_table[:].indirect(offs_sb[:]))
+        gather_x(0)
+        for c in range(2):
+            round_w1(nc.scalar.copy, 0, c, 0, P // 2)
+        for t in range(PACK):
+            quantize_w1(0, t)
+            product(0, t)
+        x_code.append(keep.tile([P, S], U32, name="x_code1", tag="w1_bf0", align_bytes=64))
+        gather_x(1)
+        round_w1(nc.scalar.copy, 1, 0, 0, P // 2)
+        round_w1(nc.vector.tensor_copy, 1, 1, 0, 40)
+        round_w1(nc.scalar.copy, 1, 1, 40, P // 2)
+        for t in range(PACK):
+            quantize_w1(1, t)
+            product(1, t)
+
+        lp = keep.tile([P, PACK, U], F32, name="lp")
+        lev2 = keep.tile([P, PACK, U], F32, name="lev2")
+        near = keep.tile([P, PACK, U], F32, name="near")
+        both = keep.tile([P, PACK, U], F32, name="both")
+        kept = keep.tile([P, PACK, U], F32, name="kept")
+        hid_bf = keep.tile([P, U, PACK], BF16, name="hid_bf", align_bytes=64)
+        hid_code = keep.tile([P, U], U32, name="hid_code", align_bytes=64)
+        hid_scale = keep.tile([P, U], U8, name="hid_scale", align_bytes=64)
+        w2_bf = keep.tile([P, N, PACK], BF16, name="w2_bf", align_bytes=64)
+        w2_code = keep.tile([P, N], U32, name="w2_code", align_bytes=64)
+        w2_scale = keep.tile([P, N], U8, name="w2_scale", align_bytes=64)
+        out_sb = keep.tile([P, U], F32, name="out_sb")
+        staged = [keep.tile([P, V, 2], F32, name=f"staged{t}") for t in STAGED]
+
+        nodes = BANK // D
+
+        def pool_cells(t):
+            if t in STAGED:
+                first = staged[STAGED.index(t)]
+                pairs = lev1[t][:, V:].rearrange("p (v e) -> p v e", e=2)
+                for h in range(halves):
+                    cells = y[t][h][:].rearrange("p (v d) -> p v d", d=D)
+                    vs = slice(h * nodes, (h + 1) * nodes)
+                    nc.scalar.copy(first[:, vs, :], cells[:, :, 0:2])
+                    nc.vector.tensor_tensor(pairs[:, vs, :], cells[:, :, 2:4], first[:, vs, :], ALU.max)
+                nc.vector.tensor_tensor(lev1[t][:, :V], pairs[:, :, 0], pairs[:, :, 1], ALU.max)
+            else:
+                for h in range(halves):
+                    nc.vector.tensor_reduce(
+                        lev1[t][:, h * nodes : (h + 1) * nodes],
+                        y[t][h][:].rearrange("p (v d) -> p v d", d=D),
+                        AXIS_X,
+                        ALU.max,
+                    )
+
+        def fetch_parent(t):
+            nc.scalar.activation(lp[:, t, :], lev1[t][:].indirect(par_sb[:]), COPY)
+
+        def add_own(t):
+            nc.vector.scalar_tensor_tensor(lev2[:, t, :], lod_sb[t][:], 0.7, lp[:, t, :], ALU.mult, ALU.add)
+
+        def fetch_neighbour(t, r0, n):
+            nc.scalar.activation(near[:, t, r0 : r0 + n], lev2[:, t, :].indirect(nb_sb[:, r0 // LIST : (r0 + n) // LIST]), COPY)
+
+        def smooth(ts, cols):
+            nc.vector.tensor_tensor(both[:, ts, cols], near[:, ts, cols], lev2[:, ts, cols], ALU.add)
+            nc.vector.scalar_tensor_tensor(kept[:, ts, cols], both[:, ts, cols], 0.5, lev2[:, ts, cols], ALU.mult, ALU.max)
+
+        def finish(r0, n):
+            cols = slice(r0, r0 + n)
+            nc.vector.tensor_tensor(
+                hid_bf[:, cols, :].rearrange("p (c i) t -> p c t i", i=4),
+                kept[:, :, cols].rearrange("p t (c i) -> p c t i", i=4),
+                unit_sb[:].unsqueeze(1).unsqueeze(3).to_broadcast([P, n // 4, PACK, 4]),
+                ALU.mult,
+            )
+            nc.vector.quantize_mx(
+                out=hid_code[:, cols].bitcast(FP8X4),
+                scales=hid_scale[:, cols],
+                in_=hid_bf[:, cols, :].rearrange("p r t -> p (r t)"),
+            )
+            acc = psum.tile([P, BANK], F32, name=f"acc{r0}", tag="bank")
+            nc.tensor.matmul_mx(
+                out=acc[:, :n],
+                lhsT=w2_code[:].bitcast(FP8X4),
+                lhsT_scale=w2_scale[:],
+                rhs=hid_code[:, cols].bitcast(FP8X4),
+                rhs_scale=hid_scale[:, cols],
+                start=True,
+                stop=True,
+            )
+            nc.scalar.copy(out_sb[:, cols], acc[:, :n])
+            nc.sync.dma_start(out=out[:, cols], in_=out_sb[:, cols])
+
+        nc.scalar.copy(
+            w2_bf[:].rearrange("p (c i) j -> p c j i", i=4),
+            w2_raw[:].rearrange("p j (c i) -> p c j i", i=4),
+        )
+        for t in range(PACK):
+            pool_cells(t)
+            fetch_parent(t)
+            if t > 0:
+                add_own(t - 1)
+        add_own(PACK - 1)
+        nc.vector.quantize_mx(out=w2_code[:].bitcast(FP8X4), scales=w2_scale[:], in_=w2_bf[:].rearrange("p n j -> p (n j)"))
+
+        for r0, n in CHUNKS:
+            group = SMOOTH_WIDTH // n
+            for t in range(PACK):
+                fetch_neighbour(t, r0, n)
+                if (t + 1) % group == 0:
+                    smooth(slice(t + 1 - group, t + 1), slice(r0, r0 + n))
+            finish(r0, n)

@@ -21,174 +21,177 @@ P = 128
 PACK = 4
 PASSES = K // (P * PACK)
 BANK = 512
+HALVES = S // BANK
 LIST = 16
-PAR_WINDOW = U + LIST
-STAGED = ()
-SMOOTH_WIDTH = 256
-CHUNKS = ((0, 256), (256, 128), (384, 128))
+QUADRANT = 32
+SCALE_ROWS = 4
+RUN = 4
+CHUNK = 128
+PARENT_WINDOW = U + LIST
+SCALAR_SHARE_FIRST = 88
+VECTOR_SHARE_LAST = 32
 
 
 def tile_picked_yoctree_relu_p_kernel(
     tc, x_words, x_scales, w1, lod, unit, w2, offs, par, nb, out
 ):
     nc = tc.nc
-    halves = S // BANK
 
     with ExitStack() as ctx:
         keep = ctx.enter_context(tc.tile_pool(name="keep", bufs=1))
-        psum = ctx.enter_context(tc.psum_pool(name="psum", bufs=8))
+        psum = ctx.enter_context(tc.psum_pool(name="psum", bufs=PACK * HALVES))
 
         offs_sb = keep.tile([P, S // LIST], U16, name="offs_sb")
         par_sb = keep.tile([P, U // LIST], U16, name="par_sb")
         nb_sb = keep.tile([P, U // LIST], U16, name="nb_sb")
-
         x_table = [keep.tile([P, T], I32, name=f"x_table{o}") for o in range(PASSES)]
         scale_table = keep.tile([P, T], U8, name="scale_table")
-        w1_raw = [[keep.tile([P, PACK, H // 2], F32, name=f"w1_raw{o}_{c}") for c in range(2)] for o in range(PASSES)]
+        w1_pair = [keep.tile([P, 2, H], F32, name=f"w1_pair{c}") for c in range(2)]
+        w1_half = [keep.tile([P, PACK, H // 2], F32, name=f"w1_half{c}") for c in range(2)]
         lod_sb = [keep.tile([P, U], F32, name=f"lod_sb{t}") for t in range(PACK)]
         unit_sb = keep.tile([P, PACK], F32, name="unit_sb")
         w2_raw = keep.tile([P, PACK, N], F32, name="w2_raw")
-        lev1 = [keep.tile([P, 3 * V if t in STAGED else PAR_WINDOW], F32, name=f"lev1_{t}") for t in range(PACK)]
+        lev1 = [keep.tile([P, PARENT_WINDOW], F32, name=f"lev1_{t}") for t in range(PACK)]
 
         nc.vector.memset(scale_table[:].bitcast(I32), 0)
         for t in range(PACK):
-            if t not in STAGED:
-                nc.vector.memset(lev1[t][:, V:], 0.0)
+            nc.vector.memset(lev1[t][:, V:], 0.0)
 
-        def load_x(o):
-            nc.sync.dma_start(out=x_table[o][:], in_=x_words[o].rearrange("p c r -> p (c r)").bitcast(I32))
-
-        def load_w1(o, c):
-            rows = w1[o * P * PACK : (o + 1) * P * PACK, c * (H // 2) : (c + 1) * (H // 2)]
-            nc.sync.dma_start(out=w1_raw[o][c][:], in_=rows.rearrange("(p j) c -> p j c", j=PACK))
-
+        w1_rows = w1.rearrange("(o p j) c -> o p j c", o=PASSES, j=PACK)
+        lod_rows = lod.rearrange("(p t) r -> p t r", t=PACK)
         nc.sync.dma_start(offs_sb[:], offs)
-        load_w1(0, 0)
+        nc.sync.dma_start(out=w1_pair[0][:], in_=w1_rows[0][:, 0:2, :])
         nc.sync.dma_start(out=unit_sb[:], in_=unit.rearrange("(p t) one -> p (t one)", t=PACK))
-        for q in range(4):
+        for q in range(P // QUADRANT):
             nc.sync.dma_start(
-                out=scale_table[32 * q : 32 * q + 4 * PASSES, :].bitcast(I32),
-                in_=x_scales[:, 4 * q : 4 * q + 4, :].bitcast(I32),
+                out=scale_table[QUADRANT * q : QUADRANT * q + SCALE_ROWS * PASSES, :].bitcast(I32),
+                in_=x_scales[:, SCALE_ROWS * q : SCALE_ROWS * (q + 1), :].bitcast(I32),
             )
-        load_x(0)
-        load_w1(0, 1)
-        load_x(1)
-        load_w1(1, 0)
-        load_w1(1, 1)
+        nc.sync.dma_start(out=w1_pair[1][:], in_=w1_rows[0][:, 2:4, :])
+        for o in range(PASSES):
+            nc.sync.dma_start(out=x_table[o][:], in_=x_words[o].rearrange("p c r -> p (c r)").bitcast(I32))
+        for c in range(2):
+            nc.sync.dma_start(out=w1_half[c][:], in_=w1_rows[1][:, :, c * (H // 2) : (c + 1) * (H // 2)])
         nc.sync.dma_start(out=w2_raw[:], in_=w2.rearrange("(p j) n -> p j n", j=PACK))
         nc.sync.dma_start(par_sb[:], par)
-        lod_rows = lod.rearrange("(p t) r -> p t r", t=PACK)
         for t in range(PACK):
             nc.sync.dma_start(out=lod_sb[t][:], in_=lod_rows[:, t, :])
         nc.sync.dma_start(nb_sb[:], nb)
 
         x_scale = keep.tile([P, S], U8, name="x_scale", align_bytes=64)
-        x_code = [keep.tile([P, S], U32, name="x_code0", align_bytes=64)]
         w1_bf = [keep.tile([P, PACK, P, PACK], BF16, name=f"w1_bf{o}", tag=f"w1_bf{o}", align_bytes=64) for o in range(PASSES)]
-        w1_code = [[keep.tile([P, P], U32, name=f"w1_code{o}_{t}", align_bytes=64) for t in range(PACK)] for o in range(PASSES)]
-        w1_scale = [[keep.tile([P, P], U8, name=f"w1_scale{o}_{t}", align_bytes=64) for t in range(PACK)] for o in range(PASSES)]
-        y = [[psum.tile([P, BANK], F32, name=f"y{t}_{h}", tag="bank") for h in range(halves)] for t in range(PACK)]
+        w1_code = [keep.tile([P, H], U32, name=f"w1_code{o}", align_bytes=64) for o in range(PASSES)]
+        w1_scale = [keep.tile([P, H], U8, name=f"w1_scale{o}", align_bytes=64) for o in range(PASSES)]
+        y = [[psum.tile([P, BANK], F32, name=f"y{t}_{h}", tag="bank") for h in range(HALVES)] for t in range(PACK)]
 
-        def gather_x(o):
-            nc.vector.tensor_copy(x_code[o][:], x_table[o][:].bitcast(U32).indirect(offs_sb[:]))
+        def round_pair(copy, c, m0, m1):
+            copy(
+                w1_bf[0][:, :, m0:m1, 2 * c : 2 * c + 2].rearrange("p t m j -> p m j t"),
+                w1_pair[c][:, :, PACK * m0 : PACK * m1].rearrange("p j (m t) -> p m j t", t=PACK),
+            )
 
-        def round_w1(copy, o, c, m0, m1):
+        def round_half(copy, c, m0, m1):
             base = c * (P // 2)
             copy(
-                w1_bf[o][:, :, base + m0 : base + m1, :].rearrange("p t m j -> p m j t"),
-                w1_raw[o][c][:, :, PACK * m0 : PACK * m1].rearrange("p j (m t) -> p m j t", t=PACK),
+                w1_bf[1][:, :, base + m0 : base + m1, :].rearrange("p t m j -> p m j t"),
+                w1_half[c][:, :, PACK * m0 : PACK * m1].rearrange("p j (m t) -> p m j t", t=PACK),
             )
 
-        def quantize_w1(o, t):
+        def quantize_w1(o, t0, t1):
             nc.vector.quantize_mx(
-                out=w1_code[o][t][:].bitcast(FP8X4),
-                scales=w1_scale[o][t][:],
-                in_=w1_bf[o][:, t, :, :].rearrange("p m j -> p (m j)"),
+                out=w1_code[o][:, t0 * P : t1 * P].bitcast(FP8X4),
+                scales=w1_scale[o][:, t0 * P : t1 * P],
+                in_=w1_bf[o][:, t0:t1, :, :].rearrange("p t m j -> p (t m j)"),
             )
 
-        def product(o, t):
-            for h in range(halves):
-                nc.tensor.matmul_mx(
-                    out=y[t][h][:],
-                    lhsT=w1_code[o][t][:].bitcast(FP8X4),
-                    lhsT_scale=w1_scale[o][t][:],
-                    rhs=x_code[o][:, h * BANK : (h + 1) * BANK].bitcast(FP8X4),
-                    rhs_scale=x_scale[4 * o :, h * BANK : (h + 1) * BANK],
-                    start=(o == 0),
-                    stop=(o == PASSES - 1),
-                )
+        def first_product(codes, o, t, h):
+            nc.tensor.matmul_mx(
+                out=y[t][h][:],
+                lhsT=w1_code[o][:, t * P : (t + 1) * P].bitcast(FP8X4),
+                lhsT_scale=w1_scale[o][:, t * P : (t + 1) * P],
+                rhs=codes[:, h * BANK : (h + 1) * BANK].bitcast(FP8X4),
+                rhs_scale=x_scale[SCALE_ROWS * o :, h * BANK : (h + 1) * BANK],
+                start=(o == 0),
+                stop=(o == PASSES - 1),
+            )
 
         nc.vector.tensor_copy(x_scale[:], scale_table[:].indirect(offs_sb[:]))
-        gather_x(0)
-        for c in range(2):
-            round_w1(nc.scalar.copy, 0, c, 0, P // 2)
-        for t in range(PACK):
-            quantize_w1(0, t)
-            product(0, t)
-        x_code.append(keep.tile([P, S], U32, name="x_code1", tag="w1_bf0", align_bytes=64))
-        gather_x(1)
-        round_w1(nc.scalar.copy, 1, 0, 0, P // 2)
-        round_w1(nc.vector.tensor_copy, 1, 1, 0, 40)
-        round_w1(nc.scalar.copy, 1, 1, 40, P // 2)
-        for t in range(PACK):
-            quantize_w1(1, t)
-            product(1, t)
+        round_pair(nc.scalar.copy, 0, 0, P)
+        round_pair(nc.scalar.copy, 1, 0, SCALAR_SHARE_FIRST)
+        round_pair(nc.vector.tensor_copy, 1, SCALAR_SHARE_FIRST, P)
+        quantize_w1(0, 0, PACK)
 
-        lp = keep.tile([P, PACK, U], F32, name="lp")
-        lev2 = keep.tile([P, PACK, U], F32, name="lev2")
-        near = keep.tile([P, PACK, U], F32, name="near")
-        both = keep.tile([P, PACK, U], F32, name="both")
-        kept = keep.tile([P, PACK, U], F32, name="kept")
-        hid_bf = keep.tile([P, U, PACK], BF16, name="hid_bf", align_bytes=64)
-        hid_code = keep.tile([P, U], U32, name="hid_code", align_bytes=64)
-        hid_scale = keep.tile([P, U], U8, name="hid_scale", align_bytes=64)
+        first_codes = keep.tile([P, S], U32, name="first_codes", align_bytes=64)
+        for h in range(HALVES):
+            entries = offs_sb[:, h * BANK // LIST : (h + 1) * BANK // LIST]
+            nc.vector.tensor_copy(first_codes[:, h * BANK : (h + 1) * BANK], x_table[0][:].bitcast(U32).indirect(entries))
+        for h in range(HALVES):
+            for t in range(PACK):
+                first_product(first_codes, 0, t, h)
+
+        second_codes = keep.tile([P, S], U32, name="second_codes", tag="w1_bf0", align_bytes=64)
+        nc.vector.tensor_copy(second_codes[:], x_table[1][:].bitcast(U32).indirect(offs_sb[:]))
+        round_half(nc.scalar.copy, 0, 0, P // 2)
+        round_half(nc.vector.tensor_copy, 1, 0, VECTOR_SHARE_LAST)
+        round_half(nc.scalar.copy, 1, VECTOR_SHARE_LAST, P // 2)
+        quantize_w1(1, 0, 1)
+        quantize_w1(1, 1, PACK)
+        for t in range(PACK):
+            for h in range(HALVES):
+                first_product(second_codes, 1, t, h)
+
+        sign = keep.tile([P, PACK], F32, name="sign")
+        size = keep.tile([P, PACK], F32, name="size")
+        nc.gpsimd.tensor_scalar(sign[:], unit_sb[:], 0.0, 2.0, ALU.is_ge, ALU.mult)
+        nc.gpsimd.tensor_scalar(sign[:], sign[:], 1.0, -1.0, ALU.mult, ALU.add)
+        nc.gpsimd.tensor_tensor(size[:], sign[:], unit_sb[:], ALU.mult)
+        own_factor = keep.tile([P, PACK], F32, name="own_factor")
+        nc.gpsimd.tensor_scalar(own_factor[:], size[:], 0.7, 0.0, ALU.mult, ALU.add)
+
         w2_bf = keep.tile([P, N, PACK], BF16, name="w2_bf", align_bytes=64)
         w2_code = keep.tile([P, N], U32, name="w2_code", align_bytes=64)
         w2_scale = keep.tile([P, N], U8, name="w2_scale", align_bytes=64)
-        out_sb = keep.tile([P, U], F32, name="out_sb")
-        staged = [keep.tile([P, V, 2], F32, name=f"staged{t}") for t in STAGED]
+        for j in range(PACK):
+            nc.scalar.activation(w2_bf[:, :, j], w2_raw[:, j, :], COPY, scale=sign[:, j : j + 1])
 
+        own = keep.tile([P, PACK, U], F32, name="own", tag="w1_bf1", align_bytes=64)
+        for t in range(PACK):
+            nc.gpsimd.tensor_scalar(own[:, t, :], lod_sb[t][:], own_factor[:, t : t + 1], 0.0, ALU.mult, ALU.add)
+
+        lp = keep.tile([P, PACK, U], F32, name="lp", tag="lp")
+        lev2 = keep.tile([P, PACK, U], F32, name="lev2")
         nodes = BANK // D
-
-        def pool_cells(t):
-            if t in STAGED:
-                first = staged[STAGED.index(t)]
-                pairs = lev1[t][:, V:].rearrange("p (v e) -> p v e", e=2)
-                for h in range(halves):
-                    cells = y[t][h][:].rearrange("p (v d) -> p v d", d=D)
-                    vs = slice(h * nodes, (h + 1) * nodes)
-                    nc.scalar.copy(first[:, vs, :], cells[:, :, 0:2])
-                    nc.vector.tensor_tensor(pairs[:, vs, :], cells[:, :, 2:4], first[:, vs, :], ALU.max)
-                nc.vector.tensor_tensor(lev1[t][:, :V], pairs[:, :, 0], pairs[:, :, 1], ALU.max)
-            else:
-                for h in range(halves):
-                    nc.vector.tensor_reduce(
-                        lev1[t][:, h * nodes : (h + 1) * nodes],
-                        y[t][h][:].rearrange("p (v d) -> p v d", d=D),
-                        AXIS_X,
-                        ALU.max,
-                    )
-
-        def fetch_parent(t):
+        for t in range(PACK):
+            for h in range(HALVES):
+                nc.vector.tensor_reduce(
+                    lev1[t][:, h * nodes : (h + 1) * nodes], y[t][h][:].rearrange("p (v d) -> p v d", d=D), AXIS_X, ALU.max
+                )
             nc.scalar.activation(lp[:, t, :], lev1[t][:].indirect(par_sb[:]), COPY)
 
-        def add_own(t):
-            nc.vector.scalar_tensor_tensor(lev2[:, t, :], lod_sb[t][:], 0.7, lp[:, t, :], ALU.mult, ALU.add)
+        near_first = keep.tile([P, PACK, CHUNK], F32, name="near_first")
 
-        def fetch_neighbour(t, r0, n):
-            nc.scalar.activation(near[:, t, r0 : r0 + n], lev2[:, t, :].indirect(nb_sb[:, r0 // LIST : (r0 + n) // LIST]), COPY)
+        def fetch_neighbours(near, t, r0):
+            nc.scalar.activation(near[:, t, :], lev2[:, t, :].indirect(nb_sb[:, r0 // LIST : (r0 + CHUNK) // LIST]), COPY)
 
-        def smooth(ts, cols):
-            nc.vector.tensor_tensor(both[:, ts, cols], near[:, ts, cols], lev2[:, ts, cols], ALU.add)
-            nc.vector.scalar_tensor_tensor(kept[:, ts, cols], both[:, ts, cols], 0.5, lev2[:, ts, cols], ALU.mult, ALU.max)
+        for t in range(PACK):
+            nc.vector.scalar_tensor_tensor(lev2[:, t, :], lp[:, t, :], size[:, t : t + 1], own[:, t, :], ALU.mult, ALU.add)
+            fetch_neighbours(near_first, t, 0)
+        nc.vector.quantize_mx(out=w2_code[:].bitcast(FP8X4), scales=w2_scale[:], in_=w2_bf[:].rearrange("p n j -> p (n j)"))
 
-        def finish(r0, n):
-            cols = slice(r0, r0 + n)
-            nc.vector.tensor_tensor(
-                hid_bf[:, cols, :].rearrange("p (c i) t -> p c t i", i=4),
-                kept[:, :, cols].rearrange("p t (c i) -> p c t i", i=4),
-                unit_sb[:].unsqueeze(1).unsqueeze(3).to_broadcast([P, n // 4, PACK, 4]),
-                ALU.mult,
+        both = keep.tile([P, PACK, U], F32, name="both")
+        hid_rows = keep.tile([P, PACK, U], BF16, name="hid_rows")
+        hid_bf = keep.tile([P, U, PACK], BF16, name="hid_bf", align_bytes=64)
+        hid_code = keep.tile([P, U], U32, name="hid_code", align_bytes=64)
+        hid_scale = keep.tile([P, U], U8, name="hid_scale", align_bytes=64)
+        out_sb = keep.tile([P, U], F32, name="out_sb")
+
+        def finish(near, r0):
+            cols = slice(r0, r0 + CHUNK)
+            nc.vector.tensor_tensor(both[:, :, cols], near, lev2[:, :, cols], ALU.add)
+            nc.vector.scalar_tensor_tensor(hid_rows[:, :, cols], both[:, :, cols], 0.5, lev2[:, :, cols], ALU.mult, ALU.max)
+            nc.vector.tensor_copy(
+                hid_bf[:, cols, :].rearrange("p (c i) t -> p c t i", i=RUN),
+                hid_rows[:, :, cols].rearrange("p t (c i) -> p c t i", i=RUN),
             )
             nc.vector.quantize_mx(
                 out=hid_code[:, cols].bitcast(FP8X4),
@@ -197,7 +200,7 @@ def tile_picked_yoctree_relu_p_kernel(
             )
             acc = psum.tile([P, BANK], F32, name=f"acc{r0}", tag="bank")
             nc.tensor.matmul_mx(
-                out=acc[:, :n],
+                out=acc[:, :CHUNK],
                 lhsT=w2_code[:].bitcast(FP8X4),
                 lhsT_scale=w2_scale[:],
                 rhs=hid_code[:, cols].bitcast(FP8X4),
@@ -205,25 +208,13 @@ def tile_picked_yoctree_relu_p_kernel(
                 start=True,
                 stop=True,
             )
-            nc.scalar.copy(out_sb[:, cols], acc[:, :n])
+            nc.scalar.copy(out_sb[:, cols], acc[:, :CHUNK])
             nc.sync.dma_start(out=out[:, cols], in_=out_sb[:, cols])
 
-        nc.scalar.copy(
-            w2_bf[:].rearrange("p (c i) j -> p c j i", i=4),
-            w2_raw[:].rearrange("p j (c i) -> p c j i", i=4),
-        )
-        for t in range(PACK):
-            pool_cells(t)
-            fetch_parent(t)
-            if t > 0:
-                add_own(t - 1)
-        add_own(PACK - 1)
-        nc.vector.quantize_mx(out=w2_code[:].bitcast(FP8X4), scales=w2_scale[:], in_=w2_bf[:].rearrange("p n j -> p (n j)"))
-
-        for r0, n in CHUNKS:
-            group = SMOOTH_WIDTH // n
+        finish(near_first[:], 0)
+        near_later = keep.tile([P, PACK, U - CHUNK], F32, name="near_later", tag="lp")
+        for r0 in range(CHUNK, U, CHUNK):
+            near = near_later[:, :, r0 - CHUNK : r0]
             for t in range(PACK):
-                fetch_neighbour(t, r0, n)
-                if (t + 1) % group == 0:
-                    smooth(slice(t + 1 - group, t + 1), slice(r0, r0 + n))
-            finish(r0, n)
+                fetch_neighbours(near, t, r0)
+            finish(near, r0)

@@ -26,10 +26,9 @@ LIST = 16
 QUADRANT = 32
 SCALE_ROWS = 4
 RUN = 4
-CHUNK = 128
+CHUNKS = (128, 128, 128, 128)
 PARENT_WINDOW = U + LIST
-SCALAR_SHARE_FIRST = 88
-VECTOR_SHARE_LAST = 32
+VECTOR_SHARE_LAST = 40
 
 
 def tile_picked_yoctree_relu_p_kernel(
@@ -72,11 +71,20 @@ def tile_picked_yoctree_relu_p_kernel(
             nc.sync.dma_start(out=x_table[o][:], in_=x_words[o].rearrange("p c r -> p (c r)").bitcast(I32))
         for c in range(2):
             nc.sync.dma_start(out=w1_half[c][:], in_=w1_rows[1][:, :, c * (H // 2) : (c + 1) * (H // 2)])
-        nc.sync.dma_start(out=w2_raw[:], in_=w2.rearrange("(p j) n -> p j n", j=PACK))
-        nc.sync.dma_start(par_sb[:], par)
         for t in range(PACK):
             nc.sync.dma_start(out=lod_sb[t][:], in_=lod_rows[:, t, :])
+        nc.sync.dma_start(par_sb[:], par)
+        nc.sync.dma_start(out=w2_raw[:], in_=w2.rearrange("(p j) n -> p j n", j=PACK))
         nc.sync.dma_start(nb_sb[:], nb)
+
+        sign = keep.tile([P, PACK], F32, name="sign")
+        twice_step = keep.tile([P, PACK], F32, name="twice_step")
+        parent_factor = keep.tile([P, PACK], F32, name="parent_factor")
+        own_factor = keep.tile([P, PACK], F32, name="own_factor")
+        nc.vector.tensor_scalar(twice_step[:], unit_sb[:], 0.0, 2.0, ALU.is_ge, ALU.mult)
+        nc.vector.tensor_scalar(sign[:], twice_step[:], 1.0, -1.0, ALU.mult, ALU.add)
+        nc.vector.scalar_tensor_tensor(parent_factor[:], unit_sb[:], 0.5, sign[:], ALU.mult, ALU.mult)
+        nc.vector.scalar_tensor_tensor(own_factor[:], unit_sb[:], 0.5 * 0.7, sign[:], ALU.mult, ALU.mult)
 
         x_scale = keep.tile([P, S], U8, name="x_scale", align_bytes=64)
         w1_bf = [keep.tile([P, PACK, P, PACK], BF16, name=f"w1_bf{o}", tag=f"w1_bf{o}", align_bytes=64) for o in range(PASSES)]
@@ -116,9 +124,8 @@ def tile_picked_yoctree_relu_p_kernel(
             )
 
         nc.vector.tensor_copy(x_scale[:], scale_table[:].indirect(offs_sb[:]))
-        round_pair(nc.scalar.copy, 0, 0, P)
-        round_pair(nc.scalar.copy, 1, 0, SCALAR_SHARE_FIRST)
-        round_pair(nc.vector.tensor_copy, 1, SCALAR_SHARE_FIRST, P)
+        for c in range(2):
+            round_pair(nc.scalar.copy, c, 0, P)
         quantize_w1(0, 0, PACK)
 
         first_codes = keep.tile([P, S], U32, name="first_codes", align_bytes=64)
@@ -140,23 +147,9 @@ def tile_picked_yoctree_relu_p_kernel(
             for h in range(HALVES):
                 first_product(second_codes, 1, t, h)
 
-        sign = keep.tile([P, PACK], F32, name="sign")
-        size = keep.tile([P, PACK], F32, name="size")
-        nc.gpsimd.tensor_scalar(sign[:], unit_sb[:], 0.0, 2.0, ALU.is_ge, ALU.mult)
-        nc.gpsimd.tensor_scalar(sign[:], sign[:], 1.0, -1.0, ALU.mult, ALU.add)
-        nc.gpsimd.tensor_tensor(size[:], sign[:], unit_sb[:], ALU.mult)
-        own_factor = keep.tile([P, PACK], F32, name="own_factor")
-        nc.gpsimd.tensor_scalar(own_factor[:], size[:], 0.7, 0.0, ALU.mult, ALU.add)
-
-        w2_bf = keep.tile([P, N, PACK], BF16, name="w2_bf", align_bytes=64)
-        w2_code = keep.tile([P, N], U32, name="w2_code", align_bytes=64)
-        w2_scale = keep.tile([P, N], U8, name="w2_scale", align_bytes=64)
-        for j in range(PACK):
-            nc.scalar.activation(w2_bf[:, :, j], w2_raw[:, j, :], COPY, scale=sign[:, j : j + 1])
-
-        own = keep.tile([P, PACK, U], F32, name="own", tag="w1_bf1", align_bytes=64)
+        own = keep.tile([P, PACK, U], F32, name="own")
         for t in range(PACK):
-            nc.gpsimd.tensor_scalar(own[:, t, :], lod_sb[t][:], own_factor[:, t : t + 1], 0.0, ALU.mult, ALU.add)
+            nc.scalar.activation(own[:, t, :], lod_sb[t][:], COPY, scale=own_factor[:, t : t + 1])
 
         lp = keep.tile([P, PACK, U], F32, name="lp", tag="lp")
         lev2 = keep.tile([P, PACK, U], F32, name="lev2")
@@ -168,30 +161,41 @@ def tile_picked_yoctree_relu_p_kernel(
                 )
             nc.scalar.activation(lp[:, t, :], lev1[t][:].indirect(par_sb[:]), COPY)
 
-        near_first = keep.tile([P, PACK, CHUNK], F32, name="near_first")
+        first = CHUNKS[0]
+        near_first = keep.tile([P, PACK, first], F32, name="near_first")
 
-        def fetch_neighbours(near, t, r0):
-            nc.scalar.activation(near[:, t, :], lev2[:, t, :].indirect(nb_sb[:, r0 // LIST : (r0 + CHUNK) // LIST]), COPY)
+        def fetch_neighbours(near, t, r0, n):
+            nc.scalar.activation(near[:, t, :], lev2[:, t, :].indirect(nb_sb[:, r0 // LIST : (r0 + n) // LIST]), COPY)
 
         for t in range(PACK):
-            nc.vector.scalar_tensor_tensor(lev2[:, t, :], lp[:, t, :], size[:, t : t + 1], own[:, t, :], ALU.mult, ALU.add)
-            fetch_neighbours(near_first, t, 0)
+            nc.vector.scalar_tensor_tensor(lev2[:, t, :], lp[:, t, :], parent_factor[:, t : t + 1], own[:, t, :], ALU.mult, ALU.add)
+            fetch_neighbours(near_first, t, 0, first)
+
+        w2_bf = keep.tile([P, N, PACK], BF16, name="w2_bf", align_bytes=64)
+        w2_code = keep.tile([P, N], U32, name="w2_code", align_bytes=64)
+        w2_scale = keep.tile([P, N], U8, name="w2_scale", align_bytes=64)
+        nc.vector.tensor_tensor(
+            w2_bf[:].rearrange("p (c i) j -> p c j i", i=RUN),
+            w2_raw[:].rearrange("p j (c i) -> p c j i", i=RUN),
+            sign[:].unsqueeze(1).unsqueeze(3).to_broadcast([P, N // RUN, PACK, RUN]),
+            ALU.mult,
+        )
         nc.vector.quantize_mx(out=w2_code[:].bitcast(FP8X4), scales=w2_scale[:], in_=w2_bf[:].rearrange("p n j -> p (n j)"))
 
-        both = keep.tile([P, PACK, U], F32, name="both")
-        hid_rows = keep.tile([P, PACK, U], BF16, name="hid_rows")
+        larger = keep.tile([P, PACK, U], F32, name="larger")
         hid_bf = keep.tile([P, U, PACK], BF16, name="hid_bf", align_bytes=64)
         hid_code = keep.tile([P, U], U32, name="hid_code", align_bytes=64)
         hid_scale = keep.tile([P, U], U8, name="hid_scale", align_bytes=64)
         out_sb = keep.tile([P, U], F32, name="out_sb")
 
-        def finish(near, r0):
-            cols = slice(r0, r0 + CHUNK)
-            nc.vector.tensor_tensor(both[:, :, cols], near, lev2[:, :, cols], ALU.add)
-            nc.vector.scalar_tensor_tensor(hid_rows[:, :, cols], both[:, :, cols], 0.5, lev2[:, :, cols], ALU.mult, ALU.max)
-            nc.vector.tensor_copy(
+        def finish(near, r0, n):
+            cols = slice(r0, r0 + n)
+            nc.vector.tensor_tensor(larger[:, :, cols], near, lev2[:, :, cols], ALU.max)
+            nc.vector.tensor_tensor(
                 hid_bf[:, cols, :].rearrange("p (c i) t -> p c t i", i=RUN),
-                hid_rows[:, :, cols].rearrange("p t (c i) -> p c t i", i=RUN),
+                larger[:, :, cols].rearrange("p t (c i) -> p c t i", i=RUN),
+                lev2[:, :, cols].rearrange("p t (c i) -> p c t i", i=RUN),
+                ALU.add,
             )
             nc.vector.quantize_mx(
                 out=hid_code[:, cols].bitcast(FP8X4),
@@ -200,7 +204,7 @@ def tile_picked_yoctree_relu_p_kernel(
             )
             acc = psum.tile([P, BANK], F32, name=f"acc{r0}", tag="bank")
             nc.tensor.matmul_mx(
-                out=acc[:, :CHUNK],
+                out=acc[:, :n],
                 lhsT=w2_code[:].bitcast(FP8X4),
                 lhsT_scale=w2_scale[:],
                 rhs=hid_code[:, cols].bitcast(FP8X4),
@@ -208,13 +212,15 @@ def tile_picked_yoctree_relu_p_kernel(
                 start=True,
                 stop=True,
             )
-            nc.scalar.copy(out_sb[:, cols], acc[:, :CHUNK])
+            nc.scalar.copy(out_sb[:, cols], acc[:, :n])
             nc.sync.dma_start(out=out[:, cols], in_=out_sb[:, cols])
 
-        finish(near_first[:], 0)
-        near_later = keep.tile([P, PACK, U - CHUNK], F32, name="near_later", tag="lp")
-        for r0 in range(CHUNK, U, CHUNK):
-            near = near_later[:, :, r0 - CHUNK : r0]
+        finish(near_first[:], 0, first)
+        near_later = keep.tile([P, PACK, U - first], F32, name="near_later", tag="lp")
+        r0 = first
+        for n in CHUNKS[1:]:
+            near = near_later[:, :, r0 - first : r0 - first + n]
             for t in range(PACK):
-                fetch_neighbours(near, t, r0)
-            finish(near, r0)
+                fetch_neighbours(near, t, r0, n)
+            finish(near, r0, n)
+            r0 = r0 + n

from contextlib import ExitStack

import concourse.mybir as mybir

K, T, S, D, N, H, V, U = 1024, 2048, 1024, 4, 128, 512, 256, 512

F32 = mybir.dt.float32
BF16 = mybir.dt.bfloat16
I32 = mybir.dt.int32
U32 = mybir.dt.uint32
U16 = mybir.dt.uint16
U8 = mybir.dt.uint8
FP8X4 = mybir.dt.float8_e4m3fn_x4
ALU = mybir.AluOpType
COPY = mybir.ActivationFunctionType.Copy
AXIS_X = mybir.AxisListType.X

FLOPS = 2 * K * H * S + 2 * H * N * U

P = 128
PACK = 4
PASSES = K // (P * PACK)
BANK = 512
HALVES = S // BANK
LIST = 16
QUADRANT = 32
SCALE_ROWS = 4
RUN = 4
CHUNKS = (128, 128, 128, 128)
PARENT_WINDOW = U + LIST
VECTOR_SHARE_LAST = 40


def tile_picked_yoctree_relu_p_kernel(
    tc, x_words, x_scales, w1, lod, unit, w2, offs, par, nb, out
):
    nc = tc.nc

    with ExitStack() as ctx:
        keep = ctx.enter_context(tc.tile_pool(name="keep", bufs=1))
        psum = ctx.enter_context(tc.psum_pool(name="psum", bufs=PACK * HALVES))

        offs_sb = keep.tile([P, S // LIST], U16, name="offs_sb")
        par_sb = keep.tile([P, U // LIST], U16, name="par_sb")
        nb_sb = keep.tile([P, U // LIST], U16, name="nb_sb")
        x_table = [keep.tile([P, T], I32, name=f"x_table{o}") for o in range(PASSES)]
        scale_table = keep.tile([P, T], U8, name="scale_table")
        w1_pair = [keep.tile([P, 2, H], F32, name=f"w1_pair{c}") for c in range(2)]
        w1_half = [keep.tile([P, PACK, H // 2], F32, name=f"w1_half{c}") for c in range(2)]
        lod_sb = [keep.tile([P, U], F32, name=f"lod_sb{t}") for t in range(PACK)]
        unit_sb = keep.tile([P, PACK], F32, name="unit_sb")
        w2_raw = keep.tile([P, PACK, N], F32, name="w2_raw")
        lev1 = [keep.tile([P, PARENT_WINDOW], F32, name=f"lev1_{t}") for t in range(PACK)]

        nc.vector.memset(scale_table[:].bitcast(I32), 0)
        for t in range(PACK):
            nc.vector.memset(lev1[t][:, V:], 0.0)

        w1_rows = w1.rearrange("(o p j) c -> o p j c", o=PASSES, j=PACK)
        lod_rows = lod.rearrange("(p t) r -> p t r", t=PACK)
        nc.sync.dma_start(offs_sb[:], offs)
        nc.sync.dma_start(out=w1_pair[0][:], in_=w1_rows[0][:, 0:2, :])
        nc.sync.dma_start(out=unit_sb[:], in_=unit.rearrange("(p t) one -> p (t one)", t=PACK))
        for q in range(P // QUADRANT):
            nc.sync.dma_start(
                out=scale_table[QUADRANT * q : QUADRANT * q + SCALE_ROWS * PASSES, :].bitcast(I32),
                in_=x_scales[:, SCALE_ROWS * q : SCALE_ROWS * (q + 1), :].bitcast(I32),
            )
        nc.sync.dma_start(out=w1_pair[1][:], in_=w1_rows[0][:, 2:4, :])
        for o in range(PASSES):
            nc.sync.dma_start(out=x_table[o][:], in_=x_words[o].rearrange("p c r -> p (c r)").bitcast(I32))
        for c in range(2):
            nc.sync.dma_start(out=w1_half[c][:], in_=w1_rows[1][:, :, c * (H // 2) : (c + 1) * (H // 2)])
        for t in range(PACK):
            nc.sync.dma_start(out=lod_sb[t][:], in_=lod_rows[:, t, :])
        nc.sync.dma_start(par_sb[:], par)
        nc.sync.dma_start(out=w2_raw[:], in_=w2.rearrange("(p j) n -> p j n", j=PACK))
        nc.sync.dma_start(nb_sb[:], nb)

        sign = keep.tile([P, PACK], F32, name="sign")
        twice_step = keep.tile([P, PACK], F32, name="twice_step")
        parent_factor = keep.tile([P, PACK], F32, name="parent_factor")
        own_factor = keep.tile([P, PACK], F32, name="own_factor")
        nc.vector.tensor_scalar(twice_step[:], unit_sb[:], 0.0, 2.0, ALU.is_ge, ALU.mult)
        nc.vector.tensor_scalar(sign[:], twice_step[:], 1.0, -1.0, ALU.mult, ALU.add)
        nc.vector.scalar_tensor_tensor(parent_factor[:], unit_sb[:], 0.5, sign[:], ALU.mult, ALU.mult)
        nc.vector.scalar_tensor_tensor(own_factor[:], unit_sb[:], 0.5 * 0.7, sign[:], ALU.mult, ALU.mult)

        x_scale = keep.tile([P, S], U8, name="x_scale", align_bytes=64)
        w1_bf = [keep.tile([P, PACK, P, PACK], BF16, name=f"w1_bf{o}", tag=f"w1_bf{o}", align_bytes=64) for o in range(PASSES)]
        w1_code = [keep.tile([P, H], U32, name=f"w1_code{o}", align_bytes=64) for o in range(PASSES)]
        w1_scale = [keep.tile([P, H], U8, name=f"w1_scale{o}", align_bytes=64) for o in range(PASSES)]
        y = [[psum.tile([P, BANK], F32, name=f"y{t}_{h}", tag="bank") for h in range(HALVES)] for t in range(PACK)]

        def round_pair(copy, c, m0, m1):
            copy(
                w1_bf[0][:, :, m0:m1, 2 * c : 2 * c + 2].rearrange("p t m j -> p m j t"),
                w1_pair[c][:, :, PACK * m0 : PACK * m1].rearrange("p j (m t) -> p m j t", t=PACK),
            )

        def round_half(copy, c, m0, m1):
            base = c * (P // 2)
            copy(
                w1_bf[1][:, :, base + m0 : base + m1, :].rearrange("p t m j -> p m j t"),
                w1_half[c][:, :, PACK * m0 : PACK * m1].rearrange("p j (m t) -> p m j t", t=PACK),
            )

        def quantize_w1(o, t0, t1):
            nc.vector.quantize_mx(
                out=w1_code[o][:, t0 * P : t1 * P].bitcast(FP8X4),
                scales=w1_scale[o][:, t0 * P : t1 * P],
                in_=w1_bf[o][:, t0:t1, :, :].rearrange("p t m j -> p (t m j)"),
            )

        def first_product(codes, o, t, h):
            nc.tensor.matmul_mx(
                out=y[t][h][:],
                lhsT=w1_code[o][:, t * P : (t + 1) * P].bitcast(FP8X4),
                lhsT_scale=w1_scale[o][:, t * P : (t + 1) * P],
                rhs=codes[:, h * BANK : (h + 1) * BANK].bitcast(FP8X4),
                rhs_scale=x_scale[SCALE_ROWS * o :, h * BANK : (h + 1) * BANK],
                start=(o == 0),
                stop=(o == PASSES - 1),
            )

        nc.vector.tensor_copy(x_scale[:], scale_table[:].indirect(offs_sb[:]))
        for c in range(2):
            round_pair(nc.scalar.copy, c, 0, P)
        quantize_w1(0, 0, PACK)

        first_codes = keep.tile([P, S], U32, name="first_codes", align_bytes=64)
        for h in range(HALVES):
            entries = offs_sb[:, h * BANK // LIST : (h + 1) * BANK // LIST]
            nc.vector.tensor_copy(first_codes[:, h * BANK : (h + 1) * BANK], x_table[0][:].bitcast(U32).indirect(entries))
        for h in range(HALVES):
            for t in range(PACK):
                first_product(first_codes, 0, t, h)

        second_codes = keep.tile([P, S], U32, name="second_codes", tag="w1_bf0", align_bytes=64)
        nc.vector.tensor_copy(second_codes[:], x_table[1][:].bitcast(U32).indirect(offs_sb[:]))
        round_half(nc.scalar.copy, 0, 0, P // 2)
        round_half(nc.vector.tensor_copy, 1, 0, VECTOR_SHARE_LAST)
        round_half(nc.scalar.copy, 1, VECTOR_SHARE_LAST, P // 2)
        quantize_w1(1, 0, 1)
        quantize_w1(1, 1, PACK)
        for t in range(PACK):
            for h in range(HALVES):
                first_product(second_codes, 1, t, h)

        own = keep.tile([P, PACK, U], F32, name="own")
        for t in range(PACK):
            nc.scalar.activation(own[:, t, :], lod_sb[t][:], COPY, scale=own_factor[:, t : t + 1])

        lp = keep.tile([P, PACK, U], F32, name="lp", tag="lp")
        lev2 = keep.tile([P, PACK, U], F32, name="lev2")
        nodes = BANK // D
        for t in range(PACK):
            for h in range(HALVES):
                nc.vector.tensor_reduce(
                    lev1[t][:, h * nodes : (h + 1) * nodes], y[t][h][:].rearrange("p (v d) -> p v d", d=D), AXIS_X, ALU.max
                )
            nc.scalar.activation(lp[:, t, :], lev1[t][:].indirect(par_sb[:]), COPY)

        first = CHUNKS[0]
        near_first = keep.tile([P, PACK, first], F32, name="near_first")

        def fetch_neighbours(near, t, r0, n):
            nc.scalar.activation(near[:, t, :], lev2[:, t, :].indirect(nb_sb[:, r0 // LIST : (r0 + n) // LIST]), COPY)

        for t in range(PACK):
            nc.vector.scalar_tensor_tensor(lev2[:, t, :], lp[:, t, :], parent_factor[:, t : t + 1], own[:, t, :], ALU.mult, ALU.add)
            fetch_neighbours(near_first, t, 0, first)

        w2_bf = keep.tile([P, N, PACK], BF16, name="w2_bf", align_bytes=64)
        w2_code = keep.tile([P, N], U32, name="w2_code", align_bytes=64)
        w2_scale = keep.tile([P, N], U8, name="w2_scale", align_bytes=64)
        nc.vector.tensor_tensor(
            w2_bf[:].rearrange("p (c i) j -> p c j i", i=RUN),
            w2_raw[:].rearrange("p j (c i) -> p c j i", i=RUN),
            sign[:].unsqueeze(1).unsqueeze(3).to_broadcast([P, N // RUN, PACK, RUN]),
            ALU.mult,
        )
        nc.vector.quantize_mx(out=w2_code[:].bitcast(FP8X4), scales=w2_scale[:], in_=w2_bf[:].rearrange("p n j -> p (n j)"))

        larger = keep.tile([P, PACK, U], F32, name="larger")
        hid_bf = keep.tile([P, U, PACK], BF16, name="hid_bf", align_bytes=64)
        hid_code = keep.tile([P, U], U32, name="hid_code", align_bytes=64)
        hid_scale = keep.tile([P, U], U8, name="hid_scale", align_bytes=64)
        out_sb = keep.tile([P, U], F32, name="out_sb")

        def finish(near, r0, n):
            cols = slice(r0, r0 + n)
            nc.vector.tensor_tensor(larger[:, :, cols], near, lev2[:, :, cols], ALU.max)
            nc.vector.tensor_tensor(
                hid_bf[:, cols, :].rearrange("p (c i) t -> p c t i", i=RUN),
                larger[:, :, cols].rearrange("p t (c i) -> p c t i", i=RUN),
                lev2[:, :, cols].rearrange("p t (c i) -> p c t i", i=RUN),
                ALU.add,
            )
            nc.vector.quantize_mx(
                out=hid_code[:, cols].bitcast(FP8X4),
                scales=hid_scale[:, cols],
                in_=hid_bf[:, cols, :].rearrange("p r t -> p (r t)"),
            )
            acc = psum.tile([P, BANK], F32, name=f"acc{r0}", tag="bank")
            nc.tensor.matmul_mx(
                out=acc[:, :n],
                lhsT=w2_code[:].bitcast(FP8X4),
                lhsT_scale=w2_scale[:],
                rhs=hid_code[:, cols].bitcast(FP8X4),
                rhs_scale=hid_scale[:, cols],
                start=True,
                stop=True,
            )
            nc.scalar.copy(out_sb[:, cols], acc[:, :n])
            nc.sync.dma_start(out=out[:, cols], in_=out_sb[:, cols])

        finish(near_first[:], 0, first)
        near_later = keep.tile([P, PACK, U - first], F32, name="near_later", tag="lp")
        r0 = first
        for n in CHUNKS[1:]:
            near = near_later[:, :, r0 - first : r0 - first + n]
            for t in range(PACK):
                fetch_neighbours(near, t, r0, n)
            finish(near, r0, n)
            r0 = r0 + n
